import numpy as np
import ml_dtypes


def mxq(x, axis, fmt="e4m3"):
    dtype, down = {"e4m3": (ml_dtypes.float8_e4m3fn, 7), "e5m2": (ml_dtypes.float8_e5m2, 14)}[fmt]
    v = np.moveaxis(np.asarray(x, np.float32).astype(ml_dtypes.bfloat16).astype(np.float64), axis, -1)
    blocks = v.reshape(v.shape[:-1] + (-1, 32))
    amax = np.abs(blocks).max(-1, keepdims=True)
    byte = np.maximum(np.where(amax > 0, np.frexp(amax)[1] - 1 + 127, 0) - down, 1)
    scale = np.exp2(byte - 127.0)
    codes = (blocks / scale).astype(np.float32).astype(dtype).astype(np.float64)
    return np.moveaxis((codes * scale).reshape(v.shape), -1, axis)


WIDE = False


def mx_kscale(k):
    if not WIDE:
        return np.ones(k)
    levels = np.array([10, -10, 5, -5, 0])
    if k % 512:
        return np.exp2(np.random.permutation(np.resize(levels, k // 32))).repeat(32)
    a = np.empty((k // 512, 16))
    for p in range(k // 512):
        a[p, :8] = np.random.permutation(np.resize(levels, 8))
        for g in range(8):
            far = levels[np.abs(levels - a[p, g]) >= 10]
            a[p, g + 8] = far[np.random.randint(len(far))]
    return np.exp2(a.ravel()).repeat(32)


def f64(x):
    return np.asarray(x).astype(np.float64)


def striped(idx):
    return np.tile(idx.reshape(-1, 16).T, (8, 1)).astype(np.uint16)


def unstriped(offs):
    return offs[:16].T.reshape(-1).astype(np.int64)


def striped8(idx):
    return np.concatenate([x.reshape(-1, 16).T for x in idx]).astype(np.uint16)


def runs(offs, k):
    lists = np.stack([offs[16 * r : 16 * r + 16].T.reshape(-1) for r in range(8)]).astype(np.int64)
    return lists[np.arange(k) % 512 // 64]


def pack_weight(w):
    k, n = w.shape
    w = f64(np.asarray(w, np.float32).astype(ml_dtypes.bfloat16)).reshape(k // 32, 32, n)
    amax = np.abs(w).max(1)
    byte = np.clip(np.where(amax > 0, np.frexp(amax)[1] - 1 + 127 - 7, 1), 1, 254)
    scaled = (w * np.exp2(127.0 - byte)[:, None, :]).reshape(k, n).astype(np.float32)
    words = np.ascontiguousarray(scaled.reshape(k // 512, 128, 4, n).transpose(0, 1, 3, 2)).astype(ml_dtypes.float8_e4m3fn).view(np.uint8)
    return words, np.ascontiguousarray(byte.astype(np.uint8).reshape(k // 512, 16, n))


def unpack_weight(words, scales):
    g, p, n, _ = words.shape
    vals = np.ascontiguousarray(words).view(ml_dtypes.float8_e4m3fn).astype(np.float64) * np.repeat(np.exp2(scales.astype(np.float64) - 127.0), 8, axis=1)[..., None]
    return vals.transpose(0, 1, 3, 2).reshape(g * 512, n)


E2M1 = np.array([0.0, 0.5, 1.0, 1.5, 2.0, 3.0, 4.0, 6.0, -0.0, -0.5, -1.0, -1.5, -2.0, -3.0, -4.0, -6.0])


def pack_fp4(w):
    k, n = w.shape
    w = f64(np.asarray(w, np.float32).astype(ml_dtypes.bfloat16)).reshape(k // 32, 32, n)
    amax = np.abs(w).max(1)
    mant, ex = np.frexp(amax / 6.0)
    byte = np.clip(np.where(amax > 0, np.where(mant > 0.5, ex, ex - 1) + 127, 1), 1, 254)
    scaled = (w * np.exp2(127.0 - byte)[:, None, :]).reshape(k, n).astype(np.float32)
    c = np.ascontiguousarray(scaled.reshape(k // 512, 128, 4, n).transpose(0, 1, 3, 2)).astype(ml_dtypes.float4_e2m1fn).view(np.uint8) & 0xF
    words = (c[..., 0::2] | (c[..., 1::2] << 4)).reshape(k // 512, 128, 2 * n)
    return np.ascontiguousarray(words), np.ascontiguousarray(byte.astype(np.uint8).reshape(k // 512, 16, n))


def unpack_fp4(words, scales):
    g, _, n = scales.shape
    words = np.ascontiguousarray(words).reshape(g, 128, n, 2)
    nib = np.empty((g, 128, n, 4), np.uint8)
    nib[..., 0::2] = words & 0xF
    nib[..., 1::2] = words >> 4
    vals = E2M1[nib] * np.repeat(np.exp2(scales.astype(np.float64) - 127.0), 8, axis=1)[..., None]
    return vals.transpose(0, 1, 3, 2).reshape(g * 512, n)


def sigmoid(v):
    return 1.0 / (1.0 + np.exp(-np.maximum(v, -700.0)))

def planes(y):
    n, m = y.shape
    v = y.astype(np.float32).astype(ml_dtypes.bfloat16).astype(np.float64).reshape(n // 32, 32, m)
    top = np.abs(v).max(1)
    byte = np.clip(np.where(top > 0, np.frexp(top)[1] - 1 + 127 - 7, 1), 1, 254)
    codes = (v * np.exp2(127.0 - byte)[:, None, :]).reshape(n, m).astype(np.float32).astype(ml_dtypes.float8_e4m3fn).view(np.uint8)
    words = codes.reshape(n // 512, 128, 4, m).transpose(0, 1, 3, 2)
    return np.ascontiguousarray(words), np.ascontiguousarray(byte.astype(np.uint8).reshape(n // 512, 16, m))


K, T, S, H, C = 512, 2048, 256, 512, 512


def setup_inputs():
    n = np.random.standard_normal
    s = mx_kscale(K)[:, None]
    packed_xT = pack_weight(n((K, T)) * s)
    packed_w1 = pack_fp4(n((K, H)) / np.sqrt(K) / s)
    return {
        "x_words": packed_xT[0],
        "x_scales": packed_xT[1],
        "w1_words": packed_w1[0],
        "w1_scales": packed_w1[1],
        "gs": (np.random.uniform(0.5, 1.5, (K, 1)) / s).astype(np.float32),
        "offs": striped(np.random.permutation(T)[:S]),
        "n1": striped8(np.stack([np.random.permutation(S) for _ in range(8)])),
        "n2": striped8(np.stack([np.random.permutation(S) for _ in range(8)])),
        "ca": striped(np.random.permutation(T)[:C]),
        "cb": striped(np.random.permutation(T)[:C]),
        "cd": striped(np.random.permutation(T)[:C]),
        "n3": striped8(np.stack([np.random.permutation(S) for _ in range(8)])),
        "n4": striped8(np.stack([np.random.permutation(S) for _ in range(8)])),
        "n5": striped(np.random.permutation(S)),
        "n6": striped(np.random.permutation(S)),
    }


def reference(x_words, x_scales, w1_words, w1_scales, gs, offs, n1, n2, ca, cb, cd, n3, n4, n5, n6):
    x_ca = unpack_weight(x_words, x_scales)[:, unstriped(ca)]
    xq = unpack_weight(x_words, x_scales)[:, unstriped(offs)]
    y = unpack_fp4(w1_words, w1_scales).T @ xq
    z = f64(gs) * (y * (sigmoid(y[np.arange(H)[:, None], runs(n1, H)] - (y[np.arange(H)[:, None], runs(n2, H)]))))
    zq = mxq(z, 0, "e4m3")
    a = 0.0625 * (x_ca.T @ zq)
    x_cb = unpack_weight(x_words, x_scales)[:, unstriped(cb)]
    b = 0.0625 * (x_cb.T @ zq)
    m1 = np.maximum(a, b[np.arange(C)[:, None], runs(n4, C)]) - (np.minimum(a[np.arange(C)[:, None], runs(n3, C)], b))
    x_cd = unpack_weight(x_words, x_scales)[:, unstriped(cd)]
    q = 0.0625 * (x_cd.T @ zq)
    out_0 = m1 + (sigmoid(q[:, unstriped(n6)] - q)) * (m1[:, unstriped(n5)] - m1)
    return (out_0,) + planes(out_0)

@@ -1,0 +1,282 @@
+from contextlib import ExitStack
+
+import concourse.mybir as mybir
+
+F32 = mybir.dt.float32
+BF16 = mybir.dt.bfloat16
+I32 = mybir.dt.int32
+U32 = mybir.dt.uint32
+U16 = mybir.dt.uint16
+U8 = mybir.dt.uint8
+FP8X4 = mybir.dt.float8_e4m3fn_x4
+FP4X4 = mybir.dt.float4_e2m1fn_x4
+ALU = mybir.AluOpType
+ACT = mybir.ActivationFunctionType
+
+P = 128
+PACK = 4
+T = 2048
+S = 256
+C = 512
+WIN = 512
+H = S // 2
+SCORE_SCALE = 0.0625
+
+FLOPS = 2 * 512 * 512 * 256 * 4
+
+
+def tile_picked_tricdmaxbpullbcmp_none_po_kernel(
+    tc, x_words, x_scales, w1_words, w1_scales, gs, offs, n1, n2, ca, cb, cd, n3, n4, n5, n6, out_0, out_1, out_2
+):
+    nc = tc.nc
+    with ExitStack() as ctx:
+        lists = ctx.enter_context(tc.tile_pool(name="lists", bufs=1))
+        keep = ctx.enter_context(tc.tile_pool(name="keep", bufs=1))
+        psum = ctx.enter_context(tc.psum_pool(name="psum", bufs=1))
+
+        def load_list(src, name):
+            tile = lists.tile(list(src.shape), U16, name=name)
+            nc.sync.dma_start(tile[:], src)
+            return tile
+
+        def load_scale_rows(queues, tile, src):
+            for q, queue in enumerate(queues):
+                queue.dma_start(tile[32 * q : 32 * q + 4, :].bitcast(I32), src[0, 4 * q : 4 * q + 4, :].bitcast(I32))
+
+        xw = keep.tile([P, T], U32, name="xw", align_bytes=64)
+        xs = keep.tile([P, T], U8, name="xs", align_bytes=64)
+        ww = keep.tile([P, 2 * C], U8, name="ww", align_bytes=64)
+        ws = keep.tile([P, C], U8, name="ws", align_bytes=64)
+        xs_in = keep.tile([P, T], U8, name="xs_in", align_bytes=64)
+        ws_in = keep.tile([P, C], U8, name="ws_in", align_bytes=64)
+        load_scale_rows([nc.sync, nc.scalar, nc.sync, nc.scalar], xs_in, x_scales)
+        l_offs = load_list(offs, "l_offs")
+        nc.sync.dma_start(xw[:].bitcast(I32), x_words[0].rearrange("p n r -> p (n r)").bitcast(I32))
+        load_scale_rows([nc.scalar, nc.scalar, nc.gpsimd, nc.gpsimd], ws_in, w1_scales)
+        nc.scalar.dma_start(ww[:].bitcast(I32), w1_words[0].bitcast(I32))
+        nc.vector.memset(xs[:].bitcast(I32), 0)
+        nc.vector.memset(ws[:].bitcast(I32), 0)
+        for r in range(4):
+            rows = slice(32 * r, 32 * r + 4)
+            nc.vector.tensor_copy(xs[rows, :].bitcast(I32), xs_in[rows, :].bitcast(I32))
+        for r in range(4):
+            rows = slice(32 * r, 32 * r + 4)
+            nc.scalar.copy(ws[rows, :].bitcast(U32), ws_in[rows, :].bitcast(U32))
+        l_ca = load_list(ca, "l_ca")
+        l_cb = load_list(cb, "l_cb")
+        l_n1 = load_list(n1, "l_n1")
+        l_n2 = load_list(n2, "l_n2")
+        gain = keep.tile([P, PACK], F32, name="gain")
+        nc.gpsimd.dma_start(gain[:], gs.rearrange("(p t) o -> p (t o)", t=PACK))
+        l_cd = load_list(cd, "l_cd")
+        l_n4 = load_list(n4, "l_n4")
+        l_n3 = load_list(n3, "l_n3")
+        l_n6 = load_list(n6, "l_n6")
+        l_n5 = load_list(n5, "l_n5")
+
+        wwd = keep.tile([P, 2 * C], U8, name="wwd", align_bytes=64)
+        wsd = keep.tile([P, C], U8, name="wsd", align_bytes=64)
+        nc.scalar.copy(
+            wwd[:].bitcast(U16).rearrange("p (t m) -> p t m", t=PACK),
+            ww[:].bitcast(U16).rearrange("p (m t) -> p t m", t=PACK),
+        )
+        for ts in (slice(0, 2), slice(2, 4)):
+            nc.gpsimd.tensor_copy(
+                wsd[:].rearrange("p (t m) -> p t m", t=PACK)[:, ts, :],
+                ws[:].rearrange("p (m t) -> p t m", t=PACK)[:, ts, :],
+            )
+
+        def dealt(tile):
+            return tile[:].rearrange("p (t m) -> p m t", t=PACK)
+
+        def pick(window, lst, dtype, name, tag):
+            tile = keep.tile([P, C], dtype, name=name, tag=tag, align_bytes=64)
+            nc.vector.tensor_copy(dealt(tile), window[:].indirect(lst[:]))
+            return tile
+
+        xqw = keep.tile([P, S], U32, name="xqw", align_bytes=64)
+        xqs = keep.tile([P, S], U8, name="xqs", align_bytes=64)
+        nc.vector.tensor_copy(xqs[:], xs[:].indirect(l_offs[:]))
+        nc.vector.tensor_copy(xqw[:], xw[:].indirect(l_offs[:]))
+        cas = pick(xs, l_ca, U8, "cas", "cas")
+        caw = pick(xw, l_ca, U32, "caw", "caw")
+        cbs = pick(xs, l_cb, U8, "cbs", "cbs")
+        cbw = pick(xw, l_cb, U32, "cbw", "cbw")
+
+        y = []
+        yg = keep.tile([P, PACK, S], F32, name="yg")
+        for t in range(PACK):
+            acc = psum.tile([P, S], F32, name="acc_y", tag="row", bufs=4)
+            nc.tensor.matmul_mx(
+                out=acc[:],
+                lhsT=wwd[:, 2 * P * t : 2 * P * (t + 1)].bitcast(FP4X4),
+                lhsT_scale=wsd[:, P * t : P * (t + 1)],
+                rhs=xqw[:].bitcast(FP8X4),
+                rhs_scale=xqs[:],
+                start=True,
+                stop=True,
+            )
+            win = keep.tile([P, S], F32, name=f"y{t}")
+            nc.scalar.activation(win[:], acc[:], ACT.Copy)
+            nc.gpsimd.tensor_scalar(yg[:, t, :], win[:], gain[:, t : t + 1], 1.0, ALU.mult, ALU.mult)
+            y.append(win)
+
+        def half(lst, h):
+            return lst[:, h * H // 16 : (h + 1) * H // 16]
+
+        zw = keep.tile([P, S], U32, name="zw", align_bytes=64)
+        zs = keep.tile([P, S], U8, name="zs", align_bytes=64)
+        dy = [keep.tile([P, PACK, H], F32, name=f"dy_{h}") for h in range(2)]
+        sy = [keep.tile([P, PACK, H], F32, name=f"sy_{h}") for h in range(2)]
+
+        def fetch_y(h, ts, tag):
+            y1 = keep.tile([P, len(ts), H], F32, name="y1", tag=tag + "1")
+            y2 = keep.tile([P, len(ts), H], F32, name="y2", tag=tag + "2")
+            for u, t in enumerate(ts):
+                nc.scalar.activation(y1[:, u, :], y[t][:].indirect(half(l_n1, h)), ACT.Copy)
+                nc.scalar.activation(y2[:, u, :], y[t][:].indirect(half(l_n2, h)), ACT.Copy)
+            return y1, y2
+
+        def diff_y(h, t0, pair, us):
+            nc.vector.tensor_tensor(
+                dy[h][:, t0 + us.start : t0 + us.stop, :], pair[0][:, us, :], pair[1][:, us, :], ALU.subtract
+            )
+
+        def gate_y(h, ts):
+            nc.scalar.activation(sy[h][:, ts, :], dy[h][:, ts, :], ACT.Sigmoid)
+
+        def woven(ap):
+            return ap.rearrange("p (c i) t -> p c t i", i=4)
+
+        def planes(ap):
+            return ap.rearrange("p t (c i) -> p c t i", i=4)
+
+        def make_z(h, tag):
+            cols = slice(h * H, (h + 1) * H)
+            zi = keep.tile([P, H, PACK], BF16, name=f"zi{h}", tag=tag, align_bytes=64)
+            nc.vector.tensor_tensor(woven(zi[:]), planes(yg[:, :, cols]), planes(sy[h][:]), ALU.mult)
+            nc.vector.quantize_mx(
+                out=zw[:, cols].bitcast(FP8X4), scales=zs[:, cols], in_=zi[:].rearrange("p j t -> p (j t)")
+            )
+
+        def score(acc, words, scales, t, cols):
+            nc.tensor.matmul_mx(
+                out=acc,
+                lhsT=words[:, P * t : P * (t + 1)].bitcast(FP8X4),
+                lhsT_scale=scales[:, P * t : P * (t + 1)],
+                rhs=zw[:, cols].bitcast(FP8X4),
+                rhs_scale=zs[:, cols],
+                start=True,
+                stop=True,
+            )
+
+        a = [keep.tile([P, WIN], F32, name=f"a{t}") for t in range(PACK)]
+        b = [keep.tile([P, WIN], F32, name=f"b{t}") for t in range(PACK)]
+        q = [keep.tile([P, WIN], F32, name=f"q{t}") for t in range(PACK)]
+        m1 = [keep.tile([P, WIN], F32, name=f"m1_{t}") for t in range(PACK)]
+
+        def score_ab(acc, t, h):
+            cols = slice(h * H, (h + 1) * H)
+            score(acc[:, 0, :], caw, cas, t, cols)
+            score(acc[:, 1, :], cbw, cbs, t, cols)
+
+        def empty_ab(acc, t, h):
+            cols = slice(h * H, (h + 1) * H)
+            nc.scalar.activation(b[t][:, cols], acc[:, 1, :], ACT.Copy, scale=SCORE_SCALE)
+            nc.scalar.activation(a[t][:, cols], acc[:, 0, :], ACT.Copy, scale=SCORE_SCALE)
+
+        first = fetch_y(0, range(PACK), "shared")
+        early = fetch_y(1, range(0, 2), "early")
+        diff_y(0, 0, first, slice(0, PACK))
+        gate_y(0, slice(0, PACK))
+        diff_y(1, 0, early, slice(0, 2))
+        make_z(0, "zi0")
+        last = fetch_y(1, range(2, PACK), "shared")
+        diff_y(1, 2, last, slice(0, 1))
+        gate_y(1, slice(0, PACK - 1))
+        diff_y(1, 2, last, slice(1, 2))
+        gate_y(1, slice(PACK - 1, PACK))
+        make_z(1, "late")
+        for pair in range(2):
+            acc = psum.tile([P, 2, 2, H], F32, name="acc_first", tag="first", bufs=2)
+            for u in range(2):
+                score_ab(acc[:, u], 2 * pair + u, 0)
+            for u in range(2):
+                empty_ab(acc[:, u], 2 * pair + u, 0)
+        cds = pick(xs, l_cd, U8, "cds", "zi0")
+        cdw = pick(xw, l_cd, U32, "cdw", "late")
+
+        second = []
+        third = []
+        for t in range(PACK):
+            acc = psum.tile([P, 2, H], F32, name="acc_second", tag="row", bufs=4)
+            score_ab(acc, t, 1)
+            second.append(acc)
+        for pair in range(2):
+            acc = psum.tile([P, 2, S], F32, name="acc_q", tag="q", bufs=2)
+            for u in range(2):
+                score(acc[:, u, :], cdw, cds, 2 * pair + u, slice(0, S))
+            third.append(acc)
+        for u in range(2):
+            nc.vector.tensor_scalar(q[u][:, :S], third[0][:, u, :], SCORE_SCALE, None, ALU.mult)
+
+        res = keep.tile([P, PACK, S], F32, name="res", align_bytes=64)
+        out_rows = out_0.rearrange("(p t) j -> p t j", t=PACK)
+        sq = [keep.tile([P, S], F32, name=f"sq_{t}") for t in range(PACK)]
+
+        def fetch_b(t):
+            b4 = keep.tile([P, S], F32, name="b_n4")
+            nc.scalar.activation(b4[:], b[t][:].indirect(l_n4[:]), ACT.Copy)
+            hi = keep.tile([P, S], F32, name=f"hi_{t}")
+            nc.vector.tensor_tensor(hi[:], a[t][:, :S], b4[:], ALU.max)
+            return hi
+
+        def fetch_a(t, hi):
+            a3 = keep.tile([P, S], F32, name="a_n3")
+            nc.scalar.activation(a3[:], a[t][:].indirect(l_n3[:]), ACT.Copy)
+            lo = keep.tile([P, S], F32, name=f"lo_{t}")
+            nc.vector.tensor_tensor(lo[:], a3[:], b[t][:, :S], ALU.min)
+            nc.vector.tensor_tensor(m1[t][:, :S], hi[:], lo[:], ALU.subtract)
+
+        def fetch_q(t):
+            dq = keep.tile([P, S], F32, name="dq")
+            nc.scalar.activation(dq[:], q[t][:].indirect(l_n6[:]), ACT.Copy)
+            nc.vector.tensor_tensor(dq[:], dq[:], q[t][:, :S], ALU.subtract)
+            return dq
+
+        def gate_q(t, dq):
+            nc.scalar.activation(sq[t][:], dq[:], ACT.Sigmoid)
+
+        def blend(t, parts):
+            pull = keep.tile([P, S], F32, name=f"pull_{t}")
+            stay = keep.tile([P, S], F32, name=f"stay_{t}")
+            nc.vector.scalar_tensor_tensor(stay[:], sq[t][:], 1.0, m1[t][:, :S], ALU.subtract, ALU.mult)
+            nc.vector.tensor_tensor(pull[:], m1[t][:].indirect(l_n5[:]), sq[t][:], ALU.mult)
+            for cols in parts:
+                nc.vector.tensor_tensor(res[:, t, cols], pull[:, cols], stay[:, cols], ALU.subtract)
+            nc.sync.dma_start(out_rows[:, t, :], res[:, t, :])
+
+        halves = [slice(0, H), slice(H, S)]
+        empty_ab(second[0], 0, 1)
+        fetch_a(0, fetch_b(0))
+        gate_q(0, fetch_q(0))
+        blend(0, [slice(0, S)])
+        for t in range(1, PACK):
+            if t >= 2:
+                nc.scalar.activation(q[t][:, :S], third[1][:, t - 2, :], ACT.Copy, scale=SCORE_SCALE)
+            dq = fetch_q(t)
+            empty_ab(second[t], t, 1)
+            fetch_a(t, fetch_b(t))
+            gate_q(t, dq)
+            blend(t, halves if t == PACK - 1 else [slice(0, S)])
+
+        ow = keep.tile([P, S], U32, name="ow", align_bytes=64)
+        osc = keep.tile([P, S], U8, name="osc", align_bytes=64)
+        ri = keep.tile([P, S, PACK], BF16, name="ri", align_bytes=64)
+        nc.scalar.copy(woven(ri[:, halves[0], :]), planes(res[:, :, halves[0]]))
+        nc.vector.tensor_copy(woven(ri[:, halves[1], :]), planes(res[:, :, halves[1]]))
+        nc.vector.quantize_mx(out=ow[:].bitcast(FP8X4), scales=osc[:], in_=ri[:].rearrange("p j t -> p (j t)"))
+        nc.sync.dma_start(out_1[0].rearrange("p n r -> p (n r)").bitcast(I32), ow[:].bitcast(I32))
+        for r in range(4):
+            queue = nc.sync if r % 2 else nc.scalar
+            queue.dma_start(out_2[0, 4 * r : 4 * r + 4, :].bitcast(I32), osc[32 * r : 32 * r + 4, :].bitcast(I32))

@@ -56,6 +56,9 @@ def tile_picked_tricdmaxbpullbcmp_none_po_kernel(
         nc.scalar.dma_start(ww[:].bitcast(I32), w1_words[0].bitcast(I32))
         nc.vector.memset(xs[:].bitcast(I32), 0)
         nc.vector.memset(ws[:].bitcast(I32), 0)
+        warm = keep.tile([P, 2], F32, name="warm")
+        nc.vector.memset(warm[:, 0:1], 0.0)
+        nc.scalar.activation(warm[:, 1:2], warm[:, 0:1], ACT.Sigmoid)
         for r in range(4):
             rows = slice(32 * r, 32 * r + 4)
             nc.vector.tensor_copy(xs[rows, :].bitcast(I32), xs_in[rows, :].bitcast(I32))

@@ -15,14 +15,17 @@ ACT = mybir.ActivationFunctionType
 
 P = 128
 PACK = 4
+LAST = PACK - 1
+QUADRANTS = 4
 T = 2048
 S = 256
 C = 512
-WIN = 512
-H = S // 2
+HALF = S // 2
+WINDOW = 2 * S
 SCORE_SCALE = 0.0625
 
-FLOPS = 2 * 512 * 512 * 256 * 4
+ON_SCALAR = 2
+FLOPS = 4 * 2 * 512 * 512 * 256
 
 
 def tile_picked_tricdmaxbpullbcmp_none_po_kernel(
@@ -33,6 +36,7 @@ def tile_picked_tricdmaxbpullbcmp_none_po_kernel(
         lists = ctx.enter_context(tc.tile_pool(name="lists", bufs=1))
         keep = ctx.enter_context(tc.tile_pool(name="keep", bufs=1))
         psum = ctx.enter_context(tc.psum_pool(name="psum", bufs=1))
+        halves = [slice(0, HALF), slice(HALF, S)]
 
         def load_list(src, name):
             tile = lists.tile(list(src.shape), U16, name=name)
@@ -40,113 +44,81 @@ def tile_picked_tricdmaxbpullbcmp_none_po_kernel(
             return tile
 
         def load_scale_rows(queues, tile, src):
-            for q, queue in enumerate(queues):
-                queue.dma_start(tile[32 * q : 32 * q + 4, :].bitcast(I32), src[0, 4 * q : 4 * q + 4, :].bitcast(I32))
+            for r, queue in enumerate(queues):
+                queue.dma_start(tile[32 * r : 32 * r + 4, :].bitcast(I32), src[0, 4 * r : 4 * r + 4, :].bitcast(I32))
 
-        xw = keep.tile([P, T], U32, name="xw", align_bytes=64)
-        xs = keep.tile([P, T], U8, name="xs", align_bytes=64)
-        ww = keep.tile([P, 2 * C], U8, name="ww", align_bytes=64)
-        ws = keep.tile([P, C], U8, name="ws", align_bytes=64)
-        xs_in = keep.tile([P, T], U8, name="xs_in", align_bytes=64)
-        ws_in = keep.tile([P, C], U8, name="ws_in", align_bytes=64)
-        load_scale_rows([nc.sync, nc.scalar, nc.sync, nc.scalar], xs_in, x_scales)
+        def entries(lst, cols):
+            return lst[:, cols.start // 16 : cols.stop // 16]
+
+        x_w = keep.tile([P, T], U32, name="x_w", align_bytes=64)
+        x_s = keep.tile([P, T], U8, name="x_s", align_bytes=64)
+        w_w = keep.tile([P, 2 * C], U8, name="w_w", align_bytes=64)
+        w_s = keep.tile([P, C], U8, name="w_s", align_bytes=64)
+        x_s_landing = keep.tile([P, T], U8, name="x_s_landing", align_bytes=64)
+        nc.gpsimd.memset(w_s[:].bitcast(I32), 0)
+        load_scale_rows([nc.sync, nc.scalar, nc.sync, nc.scalar], x_s_landing, x_scales)
         l_offs = load_list(offs, "l_offs")
-        nc.sync.dma_start(xw[:].bitcast(I32), x_words[0].rearrange("p n r -> p (n r)").bitcast(I32))
-        load_scale_rows([nc.scalar, nc.scalar, nc.gpsimd, nc.gpsimd], ws_in, w1_scales)
-        nc.scalar.dma_start(ww[:].bitcast(I32), w1_words[0].bitcast(I32))
-        nc.vector.memset(xs[:].bitcast(I32), 0)
-        nc.vector.memset(ws[:].bitcast(I32), 0)
+        nc.sync.dma_start(x_w[:].bitcast(I32), x_words[0].rearrange("p n r -> p (n r)").bitcast(I32))
+        nc.sync.dma_start(w_w[:].bitcast(I32), w1_words[0].bitcast(I32))
+        l_n1 = load_list(n1, "l_n1")
+        load_scale_rows([nc.sync] * QUADRANTS, w_s, w1_scales)
         warm = keep.tile([P, 2], F32, name="warm")
         nc.vector.memset(warm[:, 0:1], 0.0)
         nc.scalar.activation(warm[:, 1:2], warm[:, 0:1], ACT.Sigmoid)
-        for r in range(4):
+        nc.vector.memset(x_s[:].bitcast(I32), 0)
+        for r in range(QUADRANTS):
             rows = slice(32 * r, 32 * r + 4)
-            nc.vector.tensor_copy(xs[rows, :].bitcast(I32), xs_in[rows, :].bitcast(I32))
-        for r in range(4):
-            rows = slice(32 * r, 32 * r + 4)
-            nc.scalar.copy(ws[rows, :].bitcast(U32), ws_in[rows, :].bitcast(U32))
+            nc.vector.tensor_copy(x_s[rows, :].bitcast(I32), x_s_landing[rows, :].bitcast(I32))
         l_ca = load_list(ca, "l_ca")
-        l_cb = load_list(cb, "l_cb")
-        l_n1 = load_list(n1, "l_n1")
         l_n2 = load_list(n2, "l_n2")
-        gain = keep.tile([P, PACK], F32, name="gain")
+        l_cb = load_list(cb, "l_cb")
+        gain = keep.tile([P, PACK], F32, name="gain", tag="gain")
         nc.gpsimd.dma_start(gain[:], gs.rearrange("(p t) o -> p (t o)", t=PACK))
         l_cd = load_list(cd, "l_cd")
         l_n4 = load_list(n4, "l_n4")
-        l_n3 = load_list(n3, "l_n3")
         l_n6 = load_list(n6, "l_n6")
+        l_n3 = load_list(n3, "l_n3")
         l_n5 = load_list(n5, "l_n5")
 
-        wwd = keep.tile([P, 2 * C], U8, name="wwd", align_bytes=64)
-        wsd = keep.tile([P, C], U8, name="wsd", align_bytes=64)
-        nc.scalar.copy(
-            wwd[:].bitcast(U16).rearrange("p (t m) -> p t m", t=PACK),
-            ww[:].bitcast(U16).rearrange("p (m t) -> p t m", t=PACK),
-        )
-        for ts in (slice(0, 2), slice(2, 4)):
-            nc.gpsimd.tensor_copy(
-                wsd[:].rearrange("p (t m) -> p t m", t=PACK)[:, ts, :],
-                ws[:].rearrange("p (m t) -> p t m", t=PACK)[:, ts, :],
+        w_w_dealt = keep.tile([P, 2 * C], U8, name="w_w_dealt", align_bytes=64)
+        w_s_dealt = keep.tile([P, C], U8, name="w_s_dealt", align_bytes=64)
+        for ts in (slice(0, PACK // 2), slice(PACK // 2, PACK)):
+            nc.scalar.copy(
+                w_w_dealt[:].bitcast(U16).rearrange("p (t m) -> p t m", t=PACK)[:, ts, :],
+                w_w[:].bitcast(U16).rearrange("p (m t) -> p t m", t=PACK)[:, ts, :],
             )
-
-        def dealt(tile):
-            return tile[:].rearrange("p (t m) -> p m t", t=PACK)
+        w_s_by_tile = w_s[:].rearrange("p (m t) -> p t m", t=PACK)
+        for t in range(PACK // 2, PACK):
+            nc.gpsimd.tensor_copy(w_s_dealt[:, P * t : P * (t + 1)], w_s_by_tile[:, t, :])
 
         def pick(window, lst, dtype, name, tag):
             tile = keep.tile([P, C], dtype, name=name, tag=tag, align_bytes=64)
-            nc.vector.tensor_copy(dealt(tile), window[:].indirect(lst[:]))
+            nc.vector.tensor_copy(tile[:].rearrange("p (t m) -> p m t", t=PACK), window[:].indirect(lst[:]))
             return tile
 
-        xqw = keep.tile([P, S], U32, name="xqw", align_bytes=64)
-        xqs = keep.tile([P, S], U8, name="xqs", align_bytes=64)
-        nc.vector.tensor_copy(xqs[:], xs[:].indirect(l_offs[:]))
-        nc.vector.tensor_copy(xqw[:], xw[:].indirect(l_offs[:]))
-        cas = pick(xs, l_ca, U8, "cas", "cas")
-        caw = pick(xw, l_ca, U32, "caw", "caw")
-        cbs = pick(xs, l_cb, U8, "cbs", "cbs")
-        cbw = pick(xw, l_cb, U32, "cbw", "cbw")
+        xq_w = keep.tile([P, S], U32, name="xq_w", align_bytes=64)
+        xq_s = keep.tile([P, S], U8, name="xq_s", align_bytes=64)
+        nc.vector.tensor_copy(xq_s[:], x_s[:].indirect(l_offs[:]))
+        nc.vector.tensor_copy(xq_w[:], x_w[:].indirect(l_offs[:]))
+        nc.vector.tensor_copy(
+            w_s_dealt[:].rearrange("p (t m) -> p t m", t=PACK)[:, : PACK // 2, :], w_s_by_tile[:, : PACK // 2, :]
+        )
+        ca_w = pick(x_w, l_ca, U32, "ca_w", "ca_w")
+        ca_s = pick(x_s, l_ca, U8, "ca_s", "ca_s")
+        cb_w = pick(x_w, l_cb, U32, "cb_w", "cb_w")
+        cb_s = pick(x_s, l_cb, U8, "cb_s", "cb_s")
+        cd_s = pick(x_s, l_cd, U8, "cd_s", "cd_s")
 
-        y = []
-        yg = keep.tile([P, PACK, S], F32, name="yg")
-        for t in range(PACK):
-            acc = psum.tile([P, S], F32, name="acc_y", tag="row", bufs=4)
-            nc.tensor.matmul_mx(
-                out=acc[:],
-                lhsT=wwd[:, 2 * P * t : 2 * P * (t + 1)].bitcast(FP4X4),
-                lhsT_scale=wsd[:, P * t : P * (t + 1)],
-                rhs=xqw[:].bitcast(FP8X4),
-                rhs_scale=xqs[:],
-                start=True,
-                stop=True,
-            )
-            win = keep.tile([P, S], F32, name=f"y{t}")
-            nc.scalar.activation(win[:], acc[:], ACT.Copy)
-            nc.gpsimd.tensor_scalar(yg[:, t, :], win[:], gain[:, t : t + 1], 1.0, ALU.mult, ALU.mult)
-            y.append(win)
+        y = [keep.tile([P, S], F32, name=f"y{t}") for t in range(PACK)]
+        y_gain = keep.tile([P, PACK, S], F32, name="y_gain")
+        z_w = keep.tile([P, S], U32, name="z_w", align_bytes=64)
+        z_s = keep.tile([P, S], U8, name="z_s", align_bytes=64)
+        z_bf16 = [keep.tile([P, HALF, PACK], BF16, name=f"z_bf16_{h}", align_bytes=64) for h in range(2)]
+        y_gate = [keep.tile([P, PACK, HALF], F32, name=f"y_gate{h}", tag=f"y_gate{h}") for h in range(2)]
 
-        def half(lst, h):
-            return lst[:, h * H // 16 : (h + 1) * H // 16]
-
-        zw = keep.tile([P, S], U32, name="zw", align_bytes=64)
-        zs = keep.tile([P, S], U8, name="zs", align_bytes=64)
-        dy = [keep.tile([P, PACK, H], F32, name=f"dy_{h}") for h in range(2)]
-        sy = [keep.tile([P, PACK, H], F32, name=f"sy_{h}") for h in range(2)]
-
-        def fetch_y(h, ts, tag):
-            y1 = keep.tile([P, len(ts), H], F32, name="y1", tag=tag + "1")
-            y2 = keep.tile([P, len(ts), H], F32, name="y2", tag=tag + "2")
-            for u, t in enumerate(ts):
-                nc.scalar.activation(y1[:, u, :], y[t][:].indirect(half(l_n1, h)), ACT.Copy)
-                nc.scalar.activation(y2[:, u, :], y[t][:].indirect(half(l_n2, h)), ACT.Copy)
-            return y1, y2
-
-        def diff_y(h, t0, pair, us):
-            nc.vector.tensor_tensor(
-                dy[h][:, t0 + us.start : t0 + us.stop, :], pair[0][:, us, :], pair[1][:, us, :], ALU.subtract
-            )
-
-        def gate_y(h, ts):
-            nc.scalar.activation(sy[h][:, ts, :], dy[h][:, ts, :], ACT.Sigmoid)
+        def fetch_y(at_n1, at_n2, t, h):
+            nc.scalar.activation(at_n1, y[t][:].indirect(entries(l_n1, halves[h])), ACT.Copy)
+            nc.scalar.activation(at_n2, y[t][:].indirect(entries(l_n2, halves[h])), ACT.Copy)
 
         def woven(ap):
             return ap.rearrange("p (c i) t -> p c t i", i=4)
@@ -154,132 +126,204 @@ def tile_picked_tricdmaxbpullbcmp_none_po_kernel(
         def planes(ap):
             return ap.rearrange("p t (c i) -> p c t i", i=4)
 
-        def make_z(h, tag):
-            cols = slice(h * H, (h + 1) * H)
-            zi = keep.tile([P, H, PACK], BF16, name=f"zi{h}", tag=tag, align_bytes=64)
-            nc.vector.tensor_tensor(woven(zi[:]), planes(yg[:, :, cols]), planes(sy[h][:]), ALU.mult)
-            nc.vector.quantize_mx(
-                out=zw[:, cols].bitcast(FP8X4), scales=zs[:, cols], in_=zi[:].rearrange("p j t -> p (j t)")
+        def make_z(h):
+            nc.vector.tensor_tensor(
+                woven(z_bf16[h][:]), planes(y_gain[:, :, halves[h]]), planes(y_gate[h][:]), ALU.mult
             )
+
+        def quantize_z(h):
+            nc.vector.quantize_mx(
+                out=z_w[:, halves[h]].bitcast(FP8X4),
+                scales=z_s[:, halves[h]],
+                in_=z_bf16[h][:].rearrange("p j t -> p (j t)"),
+            )
+
+        first_n1 = keep.tile([P, PACK, HALF], F32, name="first_n1", tag="first_n1", align_bytes=64)
+        first_n2 = keep.tile([P, PACK, HALF], F32, name="first_n2", tag="first_n2")
+        for t in range(PACK):
+            acc = psum.tile([P, S], F32, name="acc_y", tag="late", bufs=4)
+            nc.tensor.matmul_mx(
+                out=acc[:],
+                lhsT=w_w_dealt[:, 2 * P * t : 2 * P * (t + 1)].bitcast(FP4X4),
+                lhsT_scale=w_s_dealt[:, P * t : P * (t + 1)],
+                rhs=xq_w[:].bitcast(FP8X4),
+                rhs_scale=xq_s[:],
+                start=True,
+                stop=True,
+            )
+            nc.scalar.activation(y[t][:], acc[:], ACT.Copy)
+            nc.gpsimd.tensor_scalar(y_gain[:, t, :], y[t][:], gain[:, t : t + 1], 1.0, ALU.mult, ALU.mult)
+            fetch_y(first_n1[:, t, :], first_n2[:, t, :], t, 0)
+        first_diff = keep.tile([P, PACK, HALF], F32, name="first_diff", tag="first_diff")
+        nc.vector.tensor_tensor(first_diff[:], first_n1[:], first_n2[:], ALU.subtract)
+        cd_w = pick(x_w, l_cd, U32, "cd_w", "first_n1")
+
+        early = keep.tile([P, 2, 2, HALF], F32, name="early")
+        for t in range(2):
+            fetch_y(early[:, 0, t, :], early[:, 1, t, :], t, 1)
+        nc.scalar.activation(y_gate[0][:], first_diff[:], ACT.Sigmoid)
+        early_diff = keep.tile([P, 2, HALF], F32, name="early_diff", tag="first_diff")
+        nc.vector.tensor_tensor(early_diff[:], early[:, 0], early[:, 1], ALU.subtract)
+        late = keep.tile([P, 2, 2, HALF], F32, name="late", tag="first_n2")
+        late_diff = [keep.tile([P, HALF], F32, name=f"late_diff{u}", tag=tag) for u, tag in enumerate(("late_diff0", "gain"))]
+        fetch_y(late[:, 0, 0, :], late[:, 1, 0, :], 2, 1)
+        nc.vector.tensor_tensor(late_diff[0][:], late[:, 0, 0, :], late[:, 1, 0, :], ALU.subtract)
+        make_z(0)
+        fetch_y(late[:, 0, 1, :], late[:, 1, 1, :], 3, 1)
+        nc.vector.tensor_tensor(late_diff[1][:], late[:, 0, 1, :], late[:, 1, 1, :], ALU.subtract)
+        quantize_z(0)
+        nc.scalar.activation(y_gate[1][:, :2, :], early_diff[:], ACT.Sigmoid)
+        for u in range(2):
+            nc.scalar.activation(y_gate[1][:, 2 + u, :], late_diff[u][:], ACT.Sigmoid)
+        make_z(1)
+        quantize_z(1)
+
+        a = [keep.tile([P, WINDOW], F32, name=f"a{t}") for t in range(PACK)]
+        b = [keep.tile([P, WINDOW], F32, name=f"b{t}") for t in range(PACK)]
+        q = [keep.tile([P, WINDOW], F32, name=f"q{t}", tag=f"q{t}") for t in range(PACK)]
 
         def score(acc, words, scales, t, cols):
             nc.tensor.matmul_mx(
                 out=acc,
                 lhsT=words[:, P * t : P * (t + 1)].bitcast(FP8X4),
                 lhsT_scale=scales[:, P * t : P * (t + 1)],
-                rhs=zw[:, cols].bitcast(FP8X4),
-                rhs_scale=zs[:, cols],
+                rhs=z_w[:, cols].bitcast(FP8X4),
+                rhs_scale=z_s[:, cols],
                 start=True,
                 stop=True,
             )
 
-        a = [keep.tile([P, WIN], F32, name=f"a{t}") for t in range(PACK)]
-        b = [keep.tile([P, WIN], F32, name=f"b{t}") for t in range(PACK)]
-        q = [keep.tile([P, WIN], F32, name=f"q{t}") for t in range(PACK)]
-        m1 = [keep.tile([P, WIN], F32, name=f"m1_{t}") for t in range(PACK)]
+        def score_baq(t, h, tag):
+            acc = psum.tile([P, 3, HALF], F32, name="acc_baq", tag=tag, bufs=4)
+            score(acc[:, 0, :], cb_w, cb_s, t, halves[h])
+            score(acc[:, 1, :], ca_w, ca_s, t, halves[h])
+            score(acc[:, 2, :], cd_w, cd_s, t, halves[h])
+            return acc
 
-        def score_ab(acc, t, h):
-            cols = slice(h * H, (h + 1) * H)
-            score(acc[:, 0, :], caw, cas, t, cols)
-            score(acc[:, 1, :], cbw, cbs, t, cols)
+        def scale_on_scalar(dst, acc):
+            nc.scalar.activation(dst, acc, ACT.Copy, scale=SCORE_SCALE)
 
-        def empty_ab(acc, t, h):
-            cols = slice(h * H, (h + 1) * H)
-            nc.scalar.activation(b[t][:, cols], acc[:, 1, :], ACT.Copy, scale=SCORE_SCALE)
-            nc.scalar.activation(a[t][:, cols], acc[:, 0, :], ACT.Copy, scale=SCORE_SCALE)
+        def scale_on_vector(dst, acc):
+            nc.vector.tensor_scalar(dst, acc, SCORE_SCALE, None, ALU.mult)
 
-        first = fetch_y(0, range(PACK), "shared")
-        early = fetch_y(1, range(0, 2), "early")
-        diff_y(0, 0, first, slice(0, PACK))
-        gate_y(0, slice(0, PACK))
-        diff_y(1, 0, early, slice(0, 2))
-        make_z(0, "zi0")
-        last = fetch_y(1, range(2, PACK), "shared")
-        diff_y(1, 2, last, slice(0, 1))
-        gate_y(1, slice(0, PACK - 1))
-        diff_y(1, 2, last, slice(1, 2))
-        gate_y(1, slice(PACK - 1, PACK))
-        make_z(1, "late")
-        for pair in range(2):
-            acc = psum.tile([P, 2, 2, H], F32, name="acc_first", tag="first", bufs=2)
-            for u in range(2):
-                score_ab(acc[:, u], 2 * pair + u, 0)
-            for u in range(2):
-                empty_ab(acc[:, u], 2 * pair + u, 0)
-        cds = pick(xs, l_cd, U8, "cds", "zi0")
-        cdw = pick(xw, l_cd, U32, "cdw", "late")
-
-        second = []
-        third = []
         for t in range(PACK):
-            acc = psum.tile([P, 2, H], F32, name="acc_second", tag="row", bufs=4)
-            score_ab(acc, t, 1)
-            second.append(acc)
-        for pair in range(2):
-            acc = psum.tile([P, 2, S], F32, name="acc_q", tag="q", bufs=2)
-            for u in range(2):
-                score(acc[:, u, :], cdw, cds, 2 * pair + u, slice(0, S))
-            third.append(acc)
-        for u in range(2):
-            nc.vector.tensor_scalar(q[u][:, :S], third[0][:, u, :], SCORE_SCALE, None, ALU.mult)
+            acc = score_baq(t, 0, "early")
+            empty = scale_on_scalar if t < ON_SCALAR else scale_on_vector
+            for u, dst in enumerate((b, a, q)):
+                empty(dst[t][:, halves[0]], acc[:, u, :])
+        acc_b0 = psum.tile([P, HALF], F32, name="acc_b0", tag="late", bufs=4)
+        score(acc_b0[:], cb_w, cb_s, 0, halves[1])
+        acc_aq0 = psum.tile([P, 2, HALF], F32, name="acc_aq0", tag="late", bufs=4)
+        score(acc_aq0[:, 0, :], ca_w, ca_s, 0, halves[1])
+        score(acc_aq0[:, 1, :], cd_w, cd_s, 0, halves[1])
+        scale_on_scalar(b[0][:, halves[1]], acc_b0[:])
+        scale_on_vector(a[0][:, halves[1]], acc_aq0[:, 0, :])
+        scale_on_vector(q[0][:, halves[1]], acc_aq0[:, 1, :])
+        second = {t: score_baq(t, 1, "late") for t in range(1, PACK)}
 
+        def empty_second(t):
+            for u, dst in enumerate((b, a, q)):
+                scale_on_vector(dst[t][:, halves[1]], second[t][:, u, :])
+
+        m1 = [keep.tile([P, WINDOW], F32, name=f"m1_{t}") for t in range(PACK)]
+        q_gate = [keep.tile([P, S], F32, name=f"q_gate{t}") for t in range(PACK)]
         res = keep.tile([P, PACK, S], F32, name="res", align_bytes=64)
         out_rows = out_0.rearrange("(p t) j -> p t j", t=PACK)
-        sq = [keep.tile([P, S], F32, name=f"sq_{t}") for t in range(PACK)]
+        made = {}
 
-        def fetch_b(t):
-            b4 = keep.tile([P, S], F32, name="b_n4")
-            nc.scalar.activation(b4[:], b[t][:].indirect(l_n4[:]), ACT.Copy)
-            hi = keep.tile([P, S], F32, name=f"hi_{t}")
-            nc.vector.tensor_tensor(hi[:], a[t][:, :S], b4[:], ALU.max)
-            return hi
+        def new(name, t):
+            made[name, t] = keep.tile([P, S], F32, name=f"{name}_{t}")
+            return made[name, t]
 
-        def fetch_a(t, hi):
-            a3 = keep.tile([P, S], F32, name="a_n3")
-            nc.scalar.activation(a3[:], a[t][:].indirect(l_n3[:]), ACT.Copy)
-            lo = keep.tile([P, S], F32, name=f"lo_{t}")
-            nc.vector.tensor_tensor(lo[:], a3[:], b[t][:, :S], ALU.min)
-            nc.vector.tensor_tensor(m1[t][:, :S], hi[:], lo[:], ALU.subtract)
+        def fetch_ba(t):
+            both = keep.tile([P, WINDOW], F32, name=f"fetched{t}", tag=f"q{t - 2}" if t >= 2 else f"fetched{t}")
+            made["b_n4", t], made["a_n3", t] = both[:, :S], both[:, S:]
+            nc.scalar.activation(both[:, :S], b[t][:].indirect(l_n4[:]), ACT.Copy)
+            nc.scalar.activation(both[:, S:], a[t][:].indirect(l_n3[:]), ACT.Copy)
 
         def fetch_q(t):
-            dq = keep.tile([P, S], F32, name="dq")
-            nc.scalar.activation(dq[:], q[t][:].indirect(l_n6[:]), ACT.Copy)
-            nc.vector.tensor_tensor(dq[:], dq[:], q[t][:, :S], ALU.subtract)
-            return dq
+            made["q_n6", t] = keep.tile([P, S], F32, name="q_n6")
+            nc.scalar.activation(made["q_n6", t][:], q[t][:].indirect(l_n6[:]), ACT.Copy)
 
-        def gate_q(t, dq):
-            nc.scalar.activation(sq[t][:], dq[:], ACT.Sigmoid)
+        def upper(t):
+            nc.vector.tensor_tensor(new("upper", t)[:], a[t][:, :S], made["b_n4", t], ALU.max)
 
-        def blend(t, parts):
-            pull = keep.tile([P, S], F32, name=f"pull_{t}")
-            stay = keep.tile([P, S], F32, name=f"stay_{t}")
-            nc.vector.scalar_tensor_tensor(stay[:], sq[t][:], 1.0, m1[t][:, :S], ALU.subtract, ALU.mult)
-            nc.vector.tensor_tensor(pull[:], m1[t][:].indirect(l_n5[:]), sq[t][:], ALU.mult)
-            for cols in parts:
-                nc.vector.tensor_tensor(res[:, t, cols], pull[:, cols], stay[:, cols], ALU.subtract)
+        def lower(t):
+            nc.vector.tensor_tensor(new("lower", t)[:], b[t][:, :S], made["a_n3", t], ALU.min)
+
+        def make_m1(t):
+            nc.vector.tensor_tensor(m1[t][:, :S], made["upper", t][:], made["lower", t][:], ALU.subtract)
+
+        def diff_q(t):
+            nc.vector.tensor_tensor(new("q_diff", t)[:], made["q_n6", t][:], q[t][:, :S], ALU.subtract)
+
+        def gate_q(t):
+            nc.scalar.activation(q_gate[t][:], made["q_diff", t][:], ACT.Sigmoid)
+
+        def pull(t):
+            nc.vector.tensor_tensor(new("pull", t)[:], m1[t][:].indirect(l_n5[:]), q_gate[t][:], ALU.mult)
+
+        def stay(t):
+            nc.vector.scalar_tensor_tensor(new("stay", t)[:], q_gate[t][:], 1.0, m1[t][:, :S], ALU.subtract, ALU.mult)
+
+        def finish(t):
+            nc.vector.tensor_tensor(res[:, t, :], made["pull", t][:], made["stay", t][:], ALU.subtract)
             nc.sync.dma_start(out_rows[:, t, :], res[:, t, :])
 
-        halves = [slice(0, H), slice(H, S)]
-        empty_ab(second[0], 0, 1)
-        fetch_a(0, fetch_b(0))
-        gate_q(0, fetch_q(0))
-        blend(0, [slice(0, S)])
-        for t in range(1, PACK):
-            if t >= 2:
-                nc.scalar.activation(q[t][:, :S], third[1][:, t - 2, :], ACT.Copy, scale=SCORE_SCALE)
-            dq = fetch_q(t)
-            empty_ab(second[t], t, 1)
-            fetch_a(t, fetch_b(t))
-            gate_q(t, dq)
-            blend(t, halves if t == PACK - 1 else [slice(0, S)])
+        fetch_ba(0)
+        fetch_q(0)
+        empty_second(1)
+        empty_second(2)
+        upper(0)
+        empty_second(3)
+        lower(0)
+        fetch_ba(1)
+        diff_q(0)
+        make_m1(0)
+        upper(1)
+        lower(1)
+        for t in range(PACK - 2):
+            gate_q(t)
+            fetch_q(t + 1)
+            fetch_ba(t + 2)
+            pull(t)
+            make_m1(t + 1)
+            diff_q(t + 1)
+            stay(t)
+            upper(t + 2)
+            if t == 0:
+                finish(t)
+            lower(t + 2)
+        gate_q(LAST - 1)
+        fetch_q(LAST)
+        finish(LAST - 2)
+        make_m1(LAST)
+        stay(LAST - 1)
+        diff_q(LAST)
+        pull(LAST - 1)
 
-        ow = keep.tile([P, S], U32, name="ow", align_bytes=64)
-        osc = keep.tile([P, S], U8, name="osc", align_bytes=64)
-        ri = keep.tile([P, S, PACK], BF16, name="ri", align_bytes=64)
-        nc.scalar.copy(woven(ri[:, halves[0], :]), planes(res[:, :, halves[0]]))
-        nc.vector.tensor_copy(woven(ri[:, halves[1], :]), planes(res[:, :, halves[1]]))
-        nc.vector.quantize_mx(out=ow[:].bitcast(FP8X4), scales=osc[:], in_=ri[:].rearrange("p j t -> p (j t)"))
-        nc.sync.dma_start(out_1[0].rearrange("p n r -> p (n r)").bitcast(I32), ow[:].bitcast(I32))
-        for r in range(4):
+        m1_n5 = keep.tile([P, S], F32, name="m1_n5")
+        move = keep.tile([P, S], F32, name="move")
+        gated = keep.tile([P, S], F32, name="gated")
+        nc.scalar.activation(m1_n5[:], m1[LAST][:].indirect(l_n5[:]), ACT.Copy)
+        gate_q(LAST)
+        nc.vector.tensor_tensor(move[:], m1_n5[:], m1[LAST][:, :S], ALU.subtract)
+        finish(LAST - 1)
+        for cols in halves:
+            nc.vector.tensor_tensor(gated[:, cols], move[:, cols], q_gate[LAST][:, cols], ALU.mult)
+        for cols in halves:
+            nc.vector.tensor_tensor(res[:, LAST, cols], gated[:, cols], m1[LAST][:, cols], ALU.add)
+        nc.sync.dma_start(out_rows[:, LAST, :], res[:, LAST, :])
+
+        out_w = keep.tile([P, S], U32, name="out_w", align_bytes=64)
+        out_s = keep.tile([P, S], U8, name="out_s", align_bytes=64)
+        res_bf16 = keep.tile([P, S, PACK], BF16, name="res_bf16", align_bytes=64)
+        nc.scalar.copy(woven(res_bf16[:, halves[0], :]), planes(res[:, :, halves[0]]))
+        nc.vector.tensor_copy(woven(res_bf16[:, halves[1], :]), planes(res[:, :, halves[1]]))
+        nc.vector.quantize_mx(
+            out=out_w[:].bitcast(FP8X4), scales=out_s[:], in_=res_bf16[:].rearrange("p j t -> p (j t)")
+        )
+        nc.sync.dma_start(out_1[0].rearrange("p n r -> p (n r)").bitcast(I32), out_w[:].bitcast(I32))
+        for r in range(QUADRANTS):
             queue = nc.sync if r % 2 else nc.scalar
-            queue.dma_start(out_2[0, 4 * r : 4 * r + 4, :].bitcast(I32), osc[32 * r : 32 * r + 4, :].bitcast(I32))
+            queue.dma_start(out_2[0, 4 * r : 4 * r + 4, :].bitcast(I32), out_s[32 * r : 32 * r + 4, :].bitcast(I32))

from contextlib import ExitStack

import concourse.mybir as mybir

F32 = mybir.dt.float32
BF16 = mybir.dt.bfloat16
I32 = mybir.dt.int32
U32 = mybir.dt.uint32
U16 = mybir.dt.uint16
U8 = mybir.dt.uint8
FP8X4 = mybir.dt.float8_e4m3fn_x4
FP4X4 = mybir.dt.float4_e2m1fn_x4
ALU = mybir.AluOpType
ACT = mybir.ActivationFunctionType

P = 128
PACK = 4
LAST = PACK - 1
QUADRANTS = 4
T = 2048
S = 256
C = 512
HALF = S // 2
WINDOW = 2 * S
SCORE_SCALE = 0.0625

ON_SCALAR = 2
FLOPS = 4 * 2 * 512 * 512 * 256


def tile_picked_tricdmaxbpullbcmp_none_po_kernel(
    tc, x_words, x_scales, w1_words, w1_scales, gs, offs, n1, n2, ca, cb, cd, n3, n4, n5, n6, out_0, out_1, out_2
):
    nc = tc.nc
    with ExitStack() as ctx:
        lists = ctx.enter_context(tc.tile_pool(name="lists", bufs=1))
        keep = ctx.enter_context(tc.tile_pool(name="keep", bufs=1))
        psum = ctx.enter_context(tc.psum_pool(name="psum", bufs=1))
        halves = [slice(0, HALF), slice(HALF, S)]

        def load_list(src, name):
            tile = lists.tile(list(src.shape), U16, name=name)
            nc.sync.dma_start(tile[:], src)
            return tile

        def load_scale_rows(queues, tile, src):
            for r, queue in enumerate(queues):
                queue.dma_start(tile[32 * r : 32 * r + 4, :].bitcast(I32), src[0, 4 * r : 4 * r + 4, :].bitcast(I32))

        def entries(lst, cols):
            return lst[:, cols.start // 16 : cols.stop // 16]

        x_w = keep.tile([P, T], U32, name="x_w", align_bytes=64)
        x_s = keep.tile([P, T], U8, name="x_s", align_bytes=64)
        w_w = keep.tile([P, 2 * C], U8, name="w_w", align_bytes=64)
        w_s = keep.tile([P, C], U8, name="w_s", align_bytes=64)
        x_s_landing = keep.tile([P, T], U8, name="x_s_landing", align_bytes=64)
        nc.gpsimd.memset(w_s[:].bitcast(I32), 0)
        load_scale_rows([nc.sync, nc.scalar, nc.sync, nc.scalar], x_s_landing, x_scales)
        l_offs = load_list(offs, "l_offs")
        nc.sync.dma_start(x_w[:].bitcast(I32), x_words[0].rearrange("p n r -> p (n r)").bitcast(I32))
        nc.sync.dma_start(w_w[:].bitcast(I32), w1_words[0].bitcast(I32))
        l_n1 = load_list(n1, "l_n1")
        load_scale_rows([nc.sync] * QUADRANTS, w_s, w1_scales)
        warm = keep.tile([P, 2], F32, name="warm")
        nc.vector.memset(warm[:, 0:1], 0.0)
        nc.scalar.activation(warm[:, 1:2], warm[:, 0:1], ACT.Sigmoid)
        nc.vector.memset(x_s[:].bitcast(I32), 0)
        for r in range(QUADRANTS):
            rows = slice(32 * r, 32 * r + 4)
            nc.vector.tensor_copy(x_s[rows, :].bitcast(I32), x_s_landing[rows, :].bitcast(I32))
        l_ca = load_list(ca, "l_ca")
        l_n2 = load_list(n2, "l_n2")
        l_cb = load_list(cb, "l_cb")
        gain = keep.tile([P, PACK], F32, name="gain", tag="gain")
        nc.gpsimd.dma_start(gain[:], gs.rearrange("(p t) o -> p (t o)", t=PACK))
        l_cd = load_list(cd, "l_cd")
        l_n4 = load_list(n4, "l_n4")
        l_n6 = load_list(n6, "l_n6")
        l_n3 = load_list(n3, "l_n3")
        l_n5 = load_list(n5, "l_n5")

        w_w_dealt = keep.tile([P, 2 * C], U8, name="w_w_dealt", align_bytes=64)
        w_s_dealt = keep.tile([P, C], U8, name="w_s_dealt", align_bytes=64)
        for ts in (slice(0, PACK // 2), slice(PACK // 2, PACK)):
            nc.scalar.copy(
                w_w_dealt[:].bitcast(U16).rearrange("p (t m) -> p t m", t=PACK)[:, ts, :],
                w_w[:].bitcast(U16).rearrange("p (m t) -> p t m", t=PACK)[:, ts, :],
            )
        w_s_by_tile = w_s[:].rearrange("p (m t) -> p t m", t=PACK)
        for t in range(PACK // 2, PACK):
            nc.gpsimd.tensor_copy(w_s_dealt[:, P * t : P * (t + 1)], w_s_by_tile[:, t, :])

        def pick(window, lst, dtype, name, tag):
            tile = keep.tile([P, C], dtype, name=name, tag=tag, align_bytes=64)
            nc.vector.tensor_copy(tile[:].rearrange("p (t m) -> p m t", t=PACK), window[:].indirect(lst[:]))
            return tile

        xq_w = keep.tile([P, S], U32, name="xq_w", align_bytes=64)
        xq_s = keep.tile([P, S], U8, name="xq_s", align_bytes=64)
        nc.vector.tensor_copy(xq_s[:], x_s[:].indirect(l_offs[:]))
        nc.vector.tensor_copy(xq_w[:], x_w[:].indirect(l_offs[:]))
        nc.vector.tensor_copy(
            w_s_dealt[:].rearrange("p (t m) -> p t m", t=PACK)[:, : PACK // 2, :], w_s_by_tile[:, : PACK // 2, :]
        )
        ca_w = pick(x_w, l_ca, U32, "ca_w", "ca_w")
        ca_s = pick(x_s, l_ca, U8, "ca_s", "ca_s")
        cb_w = pick(x_w, l_cb, U32, "cb_w", "cb_w")
        cb_s = pick(x_s, l_cb, U8, "cb_s", "cb_s")
        cd_s = pick(x_s, l_cd, U8, "cd_s", "cd_s")

        y = [keep.tile([P, S], F32, name=f"y{t}") for t in range(PACK)]
        y_gain = keep.tile([P, PACK, S], F32, name="y_gain")
        z_w = keep.tile([P, S], U32, name="z_w", align_bytes=64)
        z_s = keep.tile([P, S], U8, name="z_s", align_bytes=64)
        z_bf16 = [keep.tile([P, HALF, PACK], BF16, name=f"z_bf16_{h}", align_bytes=64) for h in range(2)]
        y_gate = [keep.tile([P, PACK, HALF], F32, name=f"y_gate{h}", tag=f"y_gate{h}") for h in range(2)]

        def fetch_y(at_n1, at_n2, t, h):
            nc.scalar.activation(at_n1, y[t][:].indirect(entries(l_n1, halves[h])), ACT.Copy)
            nc.scalar.activation(at_n2, y[t][:].indirect(entries(l_n2, halves[h])), ACT.Copy)

        def woven(ap):
            return ap.rearrange("p (c i) t -> p c t i", i=4)

        def planes(ap):
            return ap.rearrange("p t (c i) -> p c t i", i=4)

        def make_z(h):
            nc.vector.tensor_tensor(
                woven(z_bf16[h][:]), planes(y_gain[:, :, halves[h]]), planes(y_gate[h][:]), ALU.mult
            )

        def quantize_z(h):
            nc.vector.quantize_mx(
                out=z_w[:, halves[h]].bitcast(FP8X4),
                scales=z_s[:, halves[h]],
                in_=z_bf16[h][:].rearrange("p j t -> p (j t)"),
            )

        first_n1 = keep.tile([P, PACK, HALF], F32, name="first_n1", tag="first_n1", align_bytes=64)
        first_n2 = keep.tile([P, PACK, HALF], F32, name="first_n2", tag="first_n2")
        for t in range(PACK):
            acc = psum.tile([P, S], F32, name="acc_y", tag="late", bufs=4)
            nc.tensor.matmul_mx(
                out=acc[:],
                lhsT=w_w_dealt[:, 2 * P * t : 2 * P * (t + 1)].bitcast(FP4X4),
                lhsT_scale=w_s_dealt[:, P * t : P * (t + 1)],
                rhs=xq_w[:].bitcast(FP8X4),
                rhs_scale=xq_s[:],
                start=True,
                stop=True,
            )
            nc.scalar.activation(y[t][:], acc[:], ACT.Copy)
            nc.gpsimd.tensor_scalar(y_gain[:, t, :], y[t][:], gain[:, t : t + 1], 1.0, ALU.mult, ALU.mult)
            fetch_y(first_n1[:, t, :], first_n2[:, t, :], t, 0)
        first_diff = keep.tile([P, PACK, HALF], F32, name="first_diff", tag="first_diff")
        nc.vector.tensor_tensor(first_diff[:], first_n1[:], first_n2[:], ALU.subtract)
        cd_w = pick(x_w, l_cd, U32, "cd_w", "first_n1")

        early = keep.tile([P, 2, 2, HALF], F32, name="early")
        for t in range(2):
            fetch_y(early[:, 0, t, :], early[:, 1, t, :], t, 1)
        nc.scalar.activation(y_gate[0][:], first_diff[:], ACT.Sigmoid)
        early_diff = keep.tile([P, 2, HALF], F32, name="early_diff", tag="first_diff")
        nc.vector.tensor_tensor(early_diff[:], early[:, 0], early[:, 1], ALU.subtract)
        late = keep.tile([P, 2, 2, HALF], F32, name="late", tag="first_n2")
        late_diff = [keep.tile([P, HALF], F32, name=f"late_diff{u}", tag=tag) for u, tag in enumerate(("late_diff0", "gain"))]
        fetch_y(late[:, 0, 0, :], late[:, 1, 0, :], 2, 1)
        nc.vector.tensor_tensor(late_diff[0][:], late[:, 0, 0, :], late[:, 1, 0, :], ALU.subtract)
        make_z(0)
        fetch_y(late[:, 0, 1, :], late[:, 1, 1, :], 3, 1)
        nc.vector.tensor_tensor(late_diff[1][:], late[:, 0, 1, :], late[:, 1, 1, :], ALU.subtract)
        quantize_z(0)
        nc.scalar.activation(y_gate[1][:, :2, :], early_diff[:], ACT.Sigmoid)
        for u in range(2):
            nc.scalar.activation(y_gate[1][:, 2 + u, :], late_diff[u][:], ACT.Sigmoid)
        make_z(1)
        quantize_z(1)

        a = [keep.tile([P, WINDOW], F32, name=f"a{t}") for t in range(PACK)]
        b = [keep.tile([P, WINDOW], F32, name=f"b{t}") for t in range(PACK)]
        q = [keep.tile([P, WINDOW], F32, name=f"q{t}", tag=f"q{t}") for t in range(PACK)]

        def score(acc, words, scales, t, cols):
            nc.tensor.matmul_mx(
                out=acc,
                lhsT=words[:, P * t : P * (t + 1)].bitcast(FP8X4),
                lhsT_scale=scales[:, P * t : P * (t + 1)],
                rhs=z_w[:, cols].bitcast(FP8X4),
                rhs_scale=z_s[:, cols],
                start=True,
                stop=True,
            )

        def score_baq(t, h, tag):
            acc = psum.tile([P, 3, HALF], F32, name="acc_baq", tag=tag, bufs=4)
            score(acc[:, 0, :], cb_w, cb_s, t, halves[h])
            score(acc[:, 1, :], ca_w, ca_s, t, halves[h])
            score(acc[:, 2, :], cd_w, cd_s, t, halves[h])
            return acc

        def scale_on_scalar(dst, acc):
            nc.scalar.activation(dst, acc, ACT.Copy, scale=SCORE_SCALE)

        def scale_on_vector(dst, acc):
            nc.vector.tensor_scalar(dst, acc, SCORE_SCALE, None, ALU.mult)

        for t in range(PACK):
            acc = score_baq(t, 0, "early")
            empty = scale_on_scalar if t < ON_SCALAR else scale_on_vector
            for u, dst in enumerate((b, a, q)):
                empty(dst[t][:, halves[0]], acc[:, u, :])
        acc_b0 = psum.tile([P, HALF], F32, name="acc_b0", tag="late", bufs=4)
        score(acc_b0[:], cb_w, cb_s, 0, halves[1])
        acc_aq0 = psum.tile([P, 2, HALF], F32, name="acc_aq0", tag="late", bufs=4)
        score(acc_aq0[:, 0, :], ca_w, ca_s, 0, halves[1])
        score(acc_aq0[:, 1, :], cd_w, cd_s, 0, halves[1])
        scale_on_scalar(b[0][:, halves[1]], acc_b0[:])
        scale_on_vector(a[0][:, halves[1]], acc_aq0[:, 0, :])
        scale_on_vector(q[0][:, halves[1]], acc_aq0[:, 1, :])
        second = {t: score_baq(t, 1, "late") for t in range(1, PACK)}

        def empty_second(t):
            for u, dst in enumerate((b, a, q)):
                scale_on_vector(dst[t][:, halves[1]], second[t][:, u, :])

        m1 = [keep.tile([P, WINDOW], F32, name=f"m1_{t}") for t in range(PACK)]
        q_gate = [keep.tile([P, S], F32, name=f"q_gate{t}") for t in range(PACK)]
        res = keep.tile([P, PACK, S], F32, name="res", align_bytes=64)
        out_rows = out_0.rearrange("(p t) j -> p t j", t=PACK)
        made = {}

        def new(name, t):
            made[name, t] = keep.tile([P, S], F32, name=f"{name}_{t}")
            return made[name, t]

        def fetch_ba(t):
            both = keep.tile([P, WINDOW], F32, name=f"fetched{t}", tag=f"q{t - 2}" if t >= 2 else f"fetched{t}")
            made["b_n4", t], made["a_n3", t] = both[:, :S], both[:, S:]
            nc.scalar.activation(both[:, :S], b[t][:].indirect(l_n4[:]), ACT.Copy)
            nc.scalar.activation(both[:, S:], a[t][:].indirect(l_n3[:]), ACT.Copy)

        def fetch_q(t):
            made["q_n6", t] = keep.tile([P, S], F32, name="q_n6")
            nc.scalar.activation(made["q_n6", t][:], q[t][:].indirect(l_n6[:]), ACT.Copy)

        def upper(t):
            nc.vector.tensor_tensor(new("upper", t)[:], a[t][:, :S], made["b_n4", t], ALU.max)

        def lower(t):
            nc.vector.tensor_tensor(new("lower", t)[:], b[t][:, :S], made["a_n3", t], ALU.min)

        def make_m1(t):
            nc.vector.tensor_tensor(m1[t][:, :S], made["upper", t][:], made["lower", t][:], ALU.subtract)

        def diff_q(t):
            nc.vector.tensor_tensor(new("q_diff", t)[:], made["q_n6", t][:], q[t][:, :S], ALU.subtract)

        def gate_q(t):
            nc.scalar.activation(q_gate[t][:], made["q_diff", t][:], ACT.Sigmoid)

        def pull(t):
            nc.vector.tensor_tensor(new("pull", t)[:], m1[t][:].indirect(l_n5[:]), q_gate[t][:], ALU.mult)

        def stay(t):
            nc.vector.scalar_tensor_tensor(new("stay", t)[:], q_gate[t][:], 1.0, m1[t][:, :S], ALU.subtract, ALU.mult)

        def finish(t):
            nc.vector.tensor_tensor(res[:, t, :], made["pull", t][:], made["stay", t][:], ALU.subtract)
            nc.sync.dma_start(out_rows[:, t, :], res[:, t, :])

        fetch_ba(0)
        fetch_q(0)
        empty_second(1)
        empty_second(2)
        upper(0)
        empty_second(3)
        lower(0)
        fetch_ba(1)
        diff_q(0)
        make_m1(0)
        upper(1)
        lower(1)
        for t in range(PACK - 2):
            gate_q(t)
            fetch_q(t + 1)
            fetch_ba(t + 2)
            pull(t)
            make_m1(t + 1)
            diff_q(t + 1)
            stay(t)
            upper(t + 2)
            if t == 0:
                finish(t)
            lower(t + 2)
        gate_q(LAST - 1)
        fetch_q(LAST)
        finish(LAST - 2)
        make_m1(LAST)
        stay(LAST - 1)
        diff_q(LAST)
        pull(LAST - 1)

        m1_n5 = keep.tile([P, S], F32, name="m1_n5")
        move = keep.tile([P, S], F32, name="move")
        gated = keep.tile([P, S], F32, name="gated")
        nc.scalar.activation(m1_n5[:], m1[LAST][:].indirect(l_n5[:]), ACT.Copy)
        gate_q(LAST)
        nc.vector.tensor_tensor(move[:], m1_n5[:], m1[LAST][:, :S], ALU.subtract)
        finish(LAST - 1)
        for cols in halves:
            nc.vector.tensor_tensor(gated[:, cols], move[:, cols], q_gate[LAST][:, cols], ALU.mult)
        for cols in halves:
            nc.vector.tensor_tensor(res[:, LAST, cols], gated[:, cols], m1[LAST][:, cols], ALU.add)
        nc.sync.dma_start(out_rows[:, LAST, :], res[:, LAST, :])

        out_w = keep.tile([P, S], U32, name="out_w", align_bytes=64)
        out_s = keep.tile([P, S], U8, name="out_s", align_bytes=64)
        res_bf16 = keep.tile([P, S, PACK], BF16, name="res_bf16", align_bytes=64)
        nc.scalar.copy(woven(res_bf16[:, halves[0], :]), planes(res[:, :, halves[0]]))
        nc.vector.tensor_copy(woven(res_bf16[:, halves[1], :]), planes(res[:, :, halves[1]]))
        nc.vector.quantize_mx(
            out=out_w[:].bitcast(FP8X4), scales=out_s[:], in_=res_bf16[:].rearrange("p j t -> p (j t)")
        )
        nc.sync.dma_start(out_1[0].rearrange("p n r -> p (n r)").bitcast(I32), out_w[:].bitcast(I32))
        for r in range(QUADRANTS):
            queue = nc.sync if r % 2 else nc.scalar
            queue.dma_start(out_2[0, 4 * r : 4 * r + 4, :].bitcast(I32), out_s[32 * r : 32 * r + 4, :].bitcast(I32))
